import numpy as np
import ml_dtypes


def mxq(x, axis, fmt="e4m3"):
    dtype, down = {"e4m3": (ml_dtypes.float8_e4m3fn, 7), "e5m2": (ml_dtypes.float8_e5m2, 14)}[fmt]
    v = np.moveaxis(np.asarray(x, np.float32).astype(ml_dtypes.bfloat16).astype(np.float64), axis, -1)
    blocks = v.reshape(v.shape[:-1] + (-1, 32))
    amax = np.abs(blocks).max(-1, keepdims=True)
    byte = np.maximum(np.where(amax > 0, np.frexp(amax)[1] - 1 + 127, 0) - down, 1)
    scale = np.exp2(byte - 127.0)
    codes = (blocks / scale).astype(np.float32).astype(dtype).astype(np.float64)
    return np.moveaxis((codes * scale).reshape(v.shape), -1, axis)


WIDE = False


def mx_kscale(k):
    if not WIDE:
        return np.ones(k)
    levels = np.array([10, -10, 5, -5, 0])
    if k % 512:
        return np.exp2(np.random.permutation(np.resize(levels, k // 32))).repeat(32)
    a = np.empty((k // 512, 16))
    for p in range(k // 512):
        a[p, :8] = np.random.permutation(np.resize(levels, 8))
        for g in range(8):
            far = levels[np.abs(levels - a[p, g]) >= 10]
            a[p, g + 8] = far[np.random.randint(len(far))]
    return np.exp2(a.ravel()).repeat(32)


def f64(x):
    return np.asarray(x).astype(np.float64)


def striped(idx):
    return np.tile(np.asarray(idx).reshape(-1, 16).T, (8, 1)).astype(np.uint16)


def unstriped(offs):
    return offs[:16].T.reshape(-1).astype(np.int64)


E2M1 = np.array([0.0, 0.5, 1.0, 1.5, 2.0, 3.0, 4.0, 6.0, -0.0, -0.5, -1.0, -1.5, -2.0, -3.0, -4.0, -6.0])


def pack_weight(w, fmt):
    k, n = w.shape
    w = f64(np.asarray(w, np.float32).astype(ml_dtypes.bfloat16)).reshape(k // 32, 32, n)
    amax = np.abs(w).max(1)
    if fmt == "e4m3":
        byte = np.frexp(amax)[1] - 1 + 127 - 7
    else:
        mant, ex = np.frexp(amax / 6.0)
        byte = np.where(mant > 0.5, ex, ex - 1) + 127
    byte = np.clip(np.where(amax > 0, byte, 1), 1, 254)
    scaled = (w * np.exp2(127.0 - byte)[:, None, :]).reshape(k, n).astype(np.float32)
    by_word = np.ascontiguousarray(scaled.reshape(k // 512, 128, 4, n).transpose(0, 1, 3, 2))
    if fmt == "e4m3":
        words = by_word.astype(ml_dtypes.float8_e4m3fn).view(np.uint8)
    else:
        c = by_word.astype(ml_dtypes.float4_e2m1fn).view(np.uint8) & 0xF
        words = (c[..., 0::2] | (c[..., 1::2] << 4)).reshape(k // 512, 128, 2 * n)
    return np.ascontiguousarray(words), np.ascontiguousarray(byte.astype(np.uint8).reshape(k // 512, 16, n))


def unpack_weight(words, scales, fmt):
    g, _, n = scales.shape
    words = np.ascontiguousarray(words).reshape(g, 128, n, -1)
    if fmt == "e4m3":
        vals = words.view(ml_dtypes.float8_e4m3fn).astype(np.float64)
    else:
        nib = np.empty((g, 128, n, 4), np.uint8)
        nib[..., 0::2] = words & 0xF
        nib[..., 1::2] = words >> 4
        vals = E2M1[nib]
    vals = vals * np.repeat(np.exp2(scales.astype(np.float64) - 127.0), 8, axis=1)[..., None]
    return vals.transpose(0, 1, 3, 2).reshape(g * 512, n)


def silu(v):
    return v / (1.0 + np.exp(-v))


D, K, R, T, I, Q, G = 512, 512, 512, 2048, 512, 128, 32


def setup_inputs():
    n = np.random.standard_normal
    idx = np.random.permutation(T)[:I]
    fd = mx_kscale(D)
    fk = mx_kscale(K)
    fi = mx_kscale(I)
    keysp = pack_weight(n((D, T)) / fd[:, None], "e4m3")
    tabp = pack_weight(n((K, T)) / fk[:, None], "e4m3")
    return {
        "query": (n((D, Q)) * 0.7 / np.sqrt(D) * fd[:, None]).astype(np.float32),
        "keys_words": keysp[0],
        "keys_scales": keysp[1],
        "tab_words": tabp[0],
        "tab_scales": tabp[1],
        "w1": (n((K, R)) * 1 / np.sqrt(K) * fk[:, None]).astype(np.float32),
        "gain": (np.random.uniform(0.7, 2.0, (R, 1))).astype(np.float32),
        "os": (np.random.uniform(4.0, 16.0, (1, I)) * fi).astype(np.float32),
        "vs": (np.random.uniform(0.5, 2.0, (1, I)) / fi).astype(np.float32),
        "offs": striped(idx),
    }


def reference(query, keys_words, keys_scales, tab_words, tab_scales, w1, gain, os, vs, offs):
    idx = unstriped(offs)
    keysu = unpack_weight(keys_words, keys_scales, "e4m3")
    tabu = unpack_weight(tab_words, tab_scales, "e4m3")
    queryq = mxq(f64(query), 0, "e4m3")
    keysidxg = keysu[:, idx]
    a = queryq.T @ keysidxg
    p = np.exp(a - np.max(a, axis=1, keepdims=True))
    z = np.sum(p, axis=1, keepdims=True)
    w = p / z
    w1q = mxq(f64(w1), 0, "e4m3")
    tabidxg = tabu[:, idx]
    zh = w1q.T @ tabidxg
    mz = np.sqrt(np.square(zh).reshape(R, G, I // G).mean(axis=2) + 0.1)
    mzr = np.repeat(mz, I // G, axis=1)
    hv = silu(zh / mzr * f64(gain))
    wo1 = w * f64(os)
    wt1 = wo1.T
    hw = hv * f64(vs)
    ht1 = hw.T
    wt1q = mxq(wt1, 0, "e4m3")
    ht1q = mxq(ht1, 0, "e4m3")
    o = wt1q.T @ ht1q
    return o

@@ -1,0 +1,185 @@
+from contextlib import ExitStack
+
+import concourse.mybir as mybir
+from concourse.masks import make_identity
+
+F32 = mybir.dt.float32
+BF16 = mybir.dt.bfloat16
+I32 = mybir.dt.int32
+U32 = mybir.dt.uint32
+U16 = mybir.dt.uint16
+U8 = mybir.dt.uint8
+FP8X4 = mybir.dt.float8_e4m3fn_x4
+ACT = mybir.ActivationFunctionType
+ALU = mybir.AluOpType
+AXIS = mybir.AxisListType
+
+P = 128
+PACK = 4
+POOL_TOKENS = 2048
+SLOTS = 512
+HIDDEN = 512
+QUERIES = 128
+PAGE = 16
+PAGES = SLOTS // PAGE
+BLOCKS = HIDDEN // P
+EPS = 0.1
+TAB_PLANE = 4
+
+FLOPS = 2 * 512 * (QUERIES * SLOTS + HIDDEN * SLOTS + QUERIES * HIDDEN)
+
+
+def tile_attend_lrscaled_soft_kernel(tc, query, keys_words, keys_scales, tab_words, tab_scales, w1, gain, slot_factor, value_scale, offs, out):
+    nc = tc.nc
+    with ExitStack() as ctx:
+        held = ctx.enter_context(tc.tile_pool(name="held", bufs=1))
+        psum = ctx.enter_context(tc.psum_pool(name="psum", bufs=1))
+
+        key_bytes = held.tile([P, POOL_TOKENS], U8, name="key_bytes", align_bytes=64)
+        tab_bytes = held.tile([P, POOL_TOKENS], U8, name="tab_bytes", align_bytes=64)
+        for plane in (key_bytes, tab_bytes):
+            nc.gpsimd.memset(plane[:, : POOL_TOKENS // 2].bitcast(I32), 0)
+            nc.vector.memset(plane[:, POOL_TOKENS // 2 :].bitcast(I32), 0)
+
+        def load_scale_rows(plane, rows, first, queues):
+            for j in range(4):
+                queues[j].dma_start(out=plane[first + j : P : 32, :].bitcast(I32), in_=rows[0, j:16:4, :].bitcast(I32))
+
+        def load_words(words, name):
+            pool_words = held.tile([P, POOL_TOKENS], U32, name=name, tag=name, align_bytes=64)
+            nc.sync.dma_start(out=pool_words[:].bitcast(I32), in_=words[0].rearrange("p n t -> p (n t)").bitcast(I32))
+            return pool_words
+
+        def load_rows(matrix, name):
+            raw = held.tile([P, PACK, matrix.shape[1]], F32, name=name)
+            nc.sync.dma_start(out=raw[:], in_=matrix.rearrange("(p j) c -> p j c", j=PACK))
+            return raw
+
+        def load_by_slot(row, name):
+            column = held.tile([P, PACK], F32, name=name)
+            nc.sync.dma_start(out=column[:], in_=row.rearrange("o (p t) -> (o p) t", t=PACK))
+            return column
+
+        half = HIDDEN // 2
+        offsets = held.tile([P, SLOTS // 16], U16, name="offsets")
+        nc.sync.dma_start(offsets[:], offs)
+        q_raw = load_rows(query, "q_raw")
+        load_scale_rows(key_bytes, keys_scales, 0, [nc.scalar, nc.scalar, nc.sync, nc.sync])
+        key_pool = load_words(keys_words, "key_pool")
+        load_scale_rows(tab_bytes, tab_scales, TAB_PLANE, [nc.sync] * 4)
+        tab_pool = load_words(tab_words, "tab_pool")
+        w_low_raw = load_rows(w1[:, :half], "w_low_raw")
+        w_high_raw = load_rows(w1[:, half:], "w_high_raw")
+        os_col = load_by_slot(slot_factor, "os_col")
+        vs_col = load_by_slot(value_scale, "vs_col")
+        gain_col = held.tile([P, BLOCKS], F32, name="gain_col")
+        with nc.allow_non_contiguous_dma(reason="one gain a partition and block"):
+            nc.sync.dma_start(out=gain_col[:], in_=gain.rearrange("(b p) o -> p (b o)", p=P))
+
+        identity = held.tile([P, P], F32, name="identity")
+        make_identity(nc, identity[:])
+
+        def grouped_tile(columns, name, slot=None):
+            return held.tile([P, columns, PACK], BF16, name=name, tag=slot or name, align_bytes=64)
+
+        def interleave(engine_copy, grouped, raw):
+            engine_copy(grouped.rearrange("p (c i) j -> p c j i", i=4), raw.rearrange("p j (c i) -> p c j i", i=4))
+
+        def scalar_cast(dst, src):
+            nc.scalar.activation(dst, src, ACT.Copy)
+
+        def quantize(grouped, name):
+            columns = grouped.shape[1]
+            codes = held.tile([P, columns], U32, name=name + "_codes", align_bytes=64)
+            plane = held.tile([P, columns], U8, name=name + "_plane", align_bytes=64)
+            nc.vector.quantize_mx(out=codes[:].bitcast(FP8X4), scales=plane[:], in_=grouped.rearrange("p c j -> p (c j)"))
+            return codes, plane
+
+        def gather(pool_tile, dtype, name, slot=None):
+            picked = held.tile([P, SLOTS], dtype, name=name, tag=slot or name, align_bytes=64)
+            nc.vector.tensor_copy(picked[:], pool_tile[:].indirect(offsets[:]))
+            return picked
+
+        key_plane = gather(key_bytes, U8, "key_plane")
+        q_grouped = grouped_tile(QUERIES, "q_grouped")
+        interleave(scalar_cast, q_grouped[:], q_raw[:])
+        q_codes, q_plane = quantize(q_grouped[:], "q")
+        key_codes = gather(key_pool, U32, "key_codes")
+        scores = psum.tile([P, SLOTS], F32, name="scores", tag="scores")
+        nc.tensor.matmul_mx(out=scores[:], lhsT=q_codes[:].bitcast(FP8X4), lhsT_scale=q_plane[:],
+                            rhs=key_codes[:].bitcast(FP8X4), rhs_scale=key_plane[:], start=True, stop=True)
+        tab_plane = gather(tab_bytes, U8, "tab_plane", "key_pool")
+        neg_max = held.tile([P, 1], F32, name="neg_max")
+        nc.vector.tensor_reduce(neg_max[:], scores[:], AXIS.X, ALU.max, negate=True)
+        probs = held.tile([P, PACK, P], F32, name="probs")
+        row_sum = held.tile([P, 1], F32, name="row_sum")
+        nc.scalar.activation(probs[:], scores[:].rearrange("p (s t) -> p t s", t=PACK), ACT.Exp, bias=neg_max[:], accum_out=row_sum[:])
+        inv_sum = held.tile([P, 1], F32, name="inv_sum")
+        nc.scalar.activation(inv_sum[:], row_sum[:], ACT.Abs_reciprocal_sqrt, scale=row_sum[:])
+
+        tab_codes = gather(tab_pool, U32, "tab_codes")
+        w_grouped = grouped_tile(HIDDEN, "w_grouped", "tab_pool")
+        w_mx = []
+        for b in range(BLOCKS):
+            raw = (w_low_raw, w_high_raw)[b // 2]
+            interleave(nc.vector.tensor_copy, w_grouped[:, b * P : (b + 1) * P], raw[:, :, (b % 2) * P : (b % 2 + 1) * P])
+            w_mx.append(quantize(w_grouped[:, b * P : (b + 1) * P], "w%d" % b))
+
+        page_mean = held.tile([P, BLOCKS, PAGES], F32, name="page_mean")
+        hidden = []
+        for b in range(BLOCKS):
+            w_codes, w_plane = w_mx[b]
+            zh = psum.tile([P, SLOTS], F32, name="zh%d" % b, tag="block%d" % b)
+            nc.tensor.matmul_mx(out=zh[:], lhsT=w_codes[:].bitcast(FP8X4), lhsT_scale=w_plane[:],
+                                rhs=tab_codes[:].bitcast(FP8X4), rhs_scale=tab_plane[TAB_PLANE:P, :], start=True, stop=True)
+            hidden.append(zh)
+            squares = held.tile([P, PAGES, PAGE], F32, name="squares%d" % b, tag="squares%d" % b, align_bytes=64)
+            nc.scalar.activation(squares[:].rearrange("p g e -> p (g e)"), zh[:], ACT.Square, scale=0.25)
+            nc.vector.tensor_reduce(page_mean[:, b, :], squares[:], AXIS.X, ALU.add)
+        inv_rms = held.tile([P, BLOCKS, PAGES], F32, name="inv_rms")
+        nc.scalar.activation(inv_rms[:], page_mean[:], ACT.Abs_reciprocal_sqrt, bias=EPS)
+        factor = held.tile([P, BLOCKS, PAGES], F32, name="factor")
+        nc.vector.tensor_tensor(factor[:], inv_rms[:], gain_col[:].unsqueeze(2).to_broadcast([P, BLOCKS, PAGES]), ALU.mult)
+
+        weights = held.tile([P, PACK, P], F32, name="weights", tag="tab_pool", align_bytes=64)
+        nc.gpsimd.tensor_scalar(weights[:], probs[:], inv_sum[:], 1.0, ALU.mult, ALU.mult)
+        weights_t = psum.tile([P, PACK, P], F32, name="weights_t", tag="weights_t")
+        for t in range(PACK):
+            nc.tensor.transpose(weights_t[:, t, :], weights[:, t, :], identity[:])
+        wt_grouped = grouped_tile(QUERIES, "wt_grouped", "squares%d" % (BLOCKS - 1))
+        nc.vector.tensor_tensor(wt_grouped[:], weights_t[:].rearrange("p t q -> p q t"),
+                                os_col[:].unsqueeze(1).to_broadcast([P, P, PACK]), ALU.mult)
+
+        turned = []
+        for b in range(BLOCKS):
+            normed = held.tile([P, PACK, PAGES, PAGE // PACK], F32, name="normed%d" % b)
+            nc.vector.tensor_tensor(
+                normed[:],
+                hidden[b][:].rearrange("p (g c t) -> p t g c", g=PAGES, t=PACK),
+                factor[:, b, :].unsqueeze(1).unsqueeze(3).to_broadcast([P, PACK, PAGES, PAGE // PACK]),
+                ALU.mult,
+            )
+            normed_t = psum.tile([P, PACK, P], F32, name="normed_t%d" % b, tag="block%d" % b)
+            for t in range(PACK):
+                nc.tensor.transpose(normed_t[:, t, :], normed[:, t].rearrange("p g c -> p (g c)"), identity[:])
+            turned.append(normed_t)
+        wt_codes, wt_plane = quantize(wt_grouped[:], "wt")
+
+        head = psum.tile([P, HIDDEN - P], F32, name="head", tag="head")
+        tail = psum.tile([P, P], F32, name="tail", tag="tail")
+        for b in range(BLOCKS):
+            activated = held.tile([P, P, PACK], F32, name="activated%d" % b)
+            nc.scalar.activation(activated[:], turned[b][:].rearrange("p t r -> p r t"), ACT.Silu)
+            ht_grouped = grouped_tile(P, "ht_grouped%d" % b)
+            nc.vector.tensor_tensor(ht_grouped[:], activated[:], vs_col[:].unsqueeze(1).to_broadcast([P, P, PACK]), ALU.mult)
+            ht_codes, ht_plane = quantize(ht_grouped[:], "ht%d" % b)
+            target = tail[:] if b == BLOCKS - 1 else head[:, b * P : (b + 1) * P]
+            nc.tensor.matmul_mx(out=target, lhsT=wt_codes[:].bitcast(FP8X4), lhsT_scale=wt_plane[:],
+                                rhs=ht_codes[:].bitcast(FP8X4), rhs_scale=ht_plane[:], start=True, stop=True)
+
+        head_out = held.tile([P, HIDDEN - P], F32, name="head_out")
+        nc.scalar.copy(head_out[:], head[:])
+        nc.sync.dma_start(out=out[:, : HIDDEN - P], in_=head_out[:])
+        tail_out = held.tile([P, P], F32, name="tail_out")
+        nc.scalar.copy(tail_out[:], tail[:])
+        nc.scalar.dma_start(out=out[:, HIDDEN - P :], in_=tail_out[:])

@@ -36,22 +36,22 @@ def tile_attend_lrscaled_soft_kernel(tc, query, keys_words, keys_scales, tab_wor
         psum = ctx.enter_context(tc.psum_pool(name="psum", bufs=1))
 
         key_bytes = held.tile([P, POOL_TOKENS], U8, name="key_bytes", align_bytes=64)
-        tab_bytes = held.tile([P, POOL_TOKENS], U8, name="tab_bytes", align_bytes=64)
-        for plane in (key_bytes, tab_bytes):
-            nc.gpsimd.memset(plane[:, : POOL_TOKENS // 2].bitcast(I32), 0)
-            nc.vector.memset(plane[:, POOL_TOKENS // 2 :].bitcast(I32), 0)
+        tab_bytes = held.tile([P, POOL_TOKENS], U8, name="tab_bytes", tag="tab_bytes", align_bytes=64)
+        nc.gpsimd.memset(key_bytes[:, : POOL_TOKENS // 2].bitcast(I32), 0)
+        nc.vector.memset(key_bytes[:, POOL_TOKENS // 2 :].bitcast(I32), 0)
+        nc.vector.memset(tab_bytes[:].bitcast(I32), 0)
 
         def load_scale_rows(plane, rows, first, queues):
             for j in range(4):
                 queues[j].dma_start(out=plane[first + j : P : 32, :].bitcast(I32), in_=rows[0, j:16:4, :].bitcast(I32))
 
         def load_words(words, name):
-            pool_words = held.tile([P, POOL_TOKENS], U32, name=name, tag=name, align_bytes=64)
+            pool_words = held.tile([P, POOL_TOKENS], U32, name=name, align_bytes=64)
             nc.sync.dma_start(out=pool_words[:].bitcast(I32), in_=words[0].rearrange("p n t -> p (n t)").bitcast(I32))
             return pool_words
 
         def load_rows(matrix, name):
-            raw = held.tile([P, PACK, matrix.shape[1]], F32, name=name)
+            raw = held.tile([P, PACK, matrix.shape[1]], F32, name=name, tag=name)
             nc.sync.dma_start(out=raw[:], in_=matrix.rearrange("(p j) c -> p j c", j=PACK))
             return raw
 
@@ -67,20 +67,20 @@ def tile_attend_lrscaled_soft_kernel(tc, query, keys_words, keys_scales, tab_wor
         load_scale_rows(key_bytes, keys_scales, 0, [nc.scalar, nc.scalar, nc.sync, nc.sync])
         key_pool = load_words(keys_words, "key_pool")
         load_scale_rows(tab_bytes, tab_scales, TAB_PLANE, [nc.sync] * 4)
-        tab_pool = load_words(tab_words, "tab_pool")
         w_low_raw = load_rows(w1[:, :half], "w_low_raw")
-        w_high_raw = load_rows(w1[:, half:], "w_high_raw")
         os_col = load_by_slot(slot_factor, "os_col")
-        vs_col = load_by_slot(value_scale, "vs_col")
+        tab_pool = load_words(tab_words, "tab_pool")
+        w_high_raw = load_rows(w1[:, half:], "w_high_raw")
         gain_col = held.tile([P, BLOCKS], F32, name="gain_col")
         with nc.allow_non_contiguous_dma(reason="one gain a partition and block"):
             nc.sync.dma_start(out=gain_col[:], in_=gain.rearrange("(b p) o -> p (b o)", p=P))
+        vs_col = load_by_slot(value_scale, "vs_col")
 
         identity = held.tile([P, P], F32, name="identity")
         make_identity(nc, identity[:])
 
-        def grouped_tile(columns, name, slot=None):
-            return held.tile([P, columns, PACK], BF16, name=name, tag=slot or name, align_bytes=64)
+        def grouped_tile(columns, name):
+            return held.tile([P, columns, PACK], BF16, name=name, tag=name, align_bytes=64)
 
         def interleave(engine_copy, grouped, raw):
             engine_copy(grouped.rearrange("p (c i) j -> p c j i", i=4), raw.rearrange("p j (c i) -> p c j i", i=4))
@@ -92,40 +92,50 @@ def tile_attend_lrscaled_soft_kernel(tc, query, keys_words, keys_scales, tab_wor
             columns = grouped.shape[1]
             codes = held.tile([P, columns], U32, name=name + "_codes", align_bytes=64)
             plane = held.tile([P, columns], U8, name=name + "_plane", align_bytes=64)
-            nc.vector.quantize_mx(out=codes[:].bitcast(FP8X4), scales=plane[:], in_=grouped.rearrange("p c j -> p (c j)"))
+            nc.vector.quantize_mx(out=codes[:].bitcast(FP8X4), scales=plane[:], in_=grouped[:].rearrange("p c j -> p (c j)"))
             return codes, plane
 
-        def gather(pool_tile, dtype, name, slot=None):
-            picked = held.tile([P, SLOTS], dtype, name=name, tag=slot or name, align_bytes=64)
+        def gather(pool_tile, dtype, name):
+            picked = held.tile([P, SLOTS], dtype, name=name, align_bytes=64)
             nc.vector.tensor_copy(picked[:], pool_tile[:].indirect(offsets[:]))
             return picked
 
         key_plane = gather(key_bytes, U8, "key_plane")
         q_grouped = grouped_tile(QUERIES, "q_grouped")
         interleave(scalar_cast, q_grouped[:], q_raw[:])
-        q_codes, q_plane = quantize(q_grouped[:], "q")
+        q_codes, q_plane = quantize(q_grouped, "q")
         key_codes = gather(key_pool, U32, "key_codes")
         scores = psum.tile([P, SLOTS], F32, name="scores", tag="scores")
         nc.tensor.matmul_mx(out=scores[:], lhsT=q_codes[:].bitcast(FP8X4), lhsT_scale=q_plane[:],
                             rhs=key_codes[:].bitcast(FP8X4), rhs_scale=key_plane[:], start=True, stop=True)
-        tab_plane = gather(tab_bytes, U8, "tab_plane", "key_pool")
-        neg_max = held.tile([P, 1], F32, name="neg_max")
+        tab_plane = gather(tab_bytes, U8, "tab_plane")
+
+        def quantize_weights(b, engine_copy):
+            raw = (w_low_raw, w_high_raw)[b // 2]
+            w_grouped = grouped_tile(P, "w_grouped%d" % b)
+            interleave(engine_copy, w_grouped[:], raw[:, :, (b % 2) * P : (b % 2 + 1) * P])
+            return quantize(w_grouped, "w%d" % b)
+
+        w_mx = [quantize_weights(b, scalar_cast) for b in range(2)]
+        neg_max = held.tile([P, 1], F32, name="neg_max", tag="tab_bytes", align_bytes=64)
         nc.vector.tensor_reduce(neg_max[:], scores[:], AXIS.X, ALU.max, negate=True)
-        probs = held.tile([P, PACK, P], F32, name="probs")
+        probs = held.tile([P, SLOTS], F32, name="probs", tag="w_low_raw")
         row_sum = held.tile([P, 1], F32, name="row_sum")
-        nc.scalar.activation(probs[:], scores[:].rearrange("p (s t) -> p t s", t=PACK), ACT.Exp, bias=neg_max[:], accum_out=row_sum[:])
+        nc.scalar.activation(probs[:], scores[:], ACT.Exp, bias=neg_max[:], accum_out=row_sum[:])
         inv_sum = held.tile([P, 1], F32, name="inv_sum")
         nc.scalar.activation(inv_sum[:], row_sum[:], ACT.Abs_reciprocal_sqrt, scale=row_sum[:])
+        os_rows = psum.tile([P, PACK, P], F32, name="os_rows", tag="os_rows")
+        for t in range(PACK):
+            nc.tensor.transpose(os_rows[:, t, :], os_col[:, t : t + 1].to_broadcast([P, P]), identity[:])
 
         tab_codes = gather(tab_pool, U32, "tab_codes")
-        w_grouped = grouped_tile(HIDDEN, "w_grouped", "tab_pool")
-        w_mx = []
-        for b in range(BLOCKS):
-            raw = (w_low_raw, w_high_raw)[b // 2]
-            interleave(nc.vector.tensor_copy, w_grouped[:, b * P : (b + 1) * P], raw[:, :, (b % 2) * P : (b % 2 + 1) * P])
-            w_mx.append(quantize(w_grouped[:, b * P : (b + 1) * P], "w%d" % b))
+        w_mx.extend(quantize_weights(b, nc.vector.tensor_copy) for b in range(2, BLOCKS))
 
-        page_mean = held.tile([P, BLOCKS, PAGES], F32, name="page_mean")
+        weights = held.tile([P, P, PACK], BF16, name="weights", tag="w_grouped2", align_bytes=64)
+        nc.vector.scalar_tensor_tensor(weights[:], probs[:].rearrange("q (p t) -> q p t", t=PACK), inv_sum[:],
+                                       os_rows[:].rearrange("q t p -> q p t"), ALU.mult, ALU.mult)
+
+        page_mean = held.tile([P, BLOCKS, PAGES], F32, name="page_mean", tag="w_grouped3", align_bytes=64)
         hidden = []
         for b in range(BLOCKS):
             w_codes, w_plane = w_mx[b]
@@ -133,53 +143,61 @@ def tile_attend_lrscaled_soft_kernel(tc, query, keys_words, keys_scales, tab_wor
             nc.tensor.matmul_mx(out=zh[:], lhsT=w_codes[:].bitcast(FP8X4), lhsT_scale=w_plane[:],
                                 rhs=tab_codes[:].bitcast(FP8X4), rhs_scale=tab_plane[TAB_PLANE:P, :], start=True, stop=True)
             hidden.append(zh)
-            squares = held.tile([P, PAGES, PAGE], F32, name="squares%d" % b, tag="squares%d" % b, align_bytes=64)
+            squares = held.tile([P, PAGES, PAGE], F32, name="squares%d" % b)
             nc.scalar.activation(squares[:].rearrange("p g e -> p (g e)"), zh[:], ACT.Square, scale=0.25)
             nc.vector.tensor_reduce(page_mean[:, b, :], squares[:], AXIS.X, ALU.add)
-        inv_rms = held.tile([P, BLOCKS, PAGES], F32, name="inv_rms")
-        nc.scalar.activation(inv_rms[:], page_mean[:], ACT.Abs_reciprocal_sqrt, bias=EPS)
-        factor = held.tile([P, BLOCKS, PAGES], F32, name="factor")
-        nc.vector.tensor_tensor(factor[:], inv_rms[:], gain_col[:].unsqueeze(2).to_broadcast([P, BLOCKS, PAGES]), ALU.mult)
 
-        weights = held.tile([P, PACK, P], F32, name="weights", tag="tab_pool", align_bytes=64)
-        nc.gpsimd.tensor_scalar(weights[:], probs[:], inv_sum[:], 1.0, ALU.mult, ALU.mult)
-        weights_t = psum.tile([P, PACK, P], F32, name="weights_t", tag="weights_t")
-        for t in range(PACK):
-            nc.tensor.transpose(weights_t[:, t, :], weights[:, t, :], identity[:])
-        wt_grouped = grouped_tile(QUERIES, "wt_grouped", "squares%d" % (BLOCKS - 1))
-        nc.vector.tensor_tensor(wt_grouped[:], weights_t[:].rearrange("p t q -> p q t"),
-                                os_col[:].unsqueeze(1).to_broadcast([P, P, PACK]), ALU.mult)
+        weight_pairs = weights[:].rearrange("q p t -> q (p t)").bitcast(F32)
+        pairs_t = psum.tile([P, 2, QUERIES], F32, name="pairs_t", tag="scores")
+        for u in range(2):
+            nc.tensor.transpose(pairs_t[:, u, :], weight_pairs[:, u : SLOTS // 2 : 2], identity[:])
+        wt_grouped = grouped_tile(QUERIES, "wt_grouped")
+        nc.scalar.copy(wt_grouped[:].bitcast(F32), pairs_t[:].rearrange("p u q -> p q u"))
+
+        inv_rms = held.tile([P, BLOCKS, PAGES, PAGE // PACK], F32, name="inv_rms")
+        for blocks in (slice(0, BLOCKS - 1), slice(BLOCKS - 1, BLOCKS)):
+            count = (blocks.stop - blocks.start) * PAGES
+            nc.scalar.activation(
+                inv_rms[:, blocks].rearrange("p b g c -> p (b g) c"),
+                page_mean[:, blocks].rearrange("p b g -> p (b g)").unsqueeze(2).to_broadcast([P, count, PAGE // PACK]),
+                ACT.Abs_reciprocal_sqrt, bias=EPS)
 
         turned = []
         for b in range(BLOCKS):
-            normed = held.tile([P, PACK, PAGES, PAGE // PACK], F32, name="normed%d" % b)
-            nc.vector.tensor_tensor(
+            normed = held.tile([P, PACK, P], F32, name="normed%d" % b)
+            nc.vector.scalar_tensor_tensor(
                 normed[:],
-                hidden[b][:].rearrange("p (g c t) -> p t g c", g=PAGES, t=PACK),
-                factor[:, b, :].unsqueeze(1).unsqueeze(3).to_broadcast([P, PACK, PAGES, PAGE // PACK]),
-                ALU.mult,
+                hidden[b][:].rearrange("p (s t) -> p t s", t=PACK),
+                gain_col[:, b : b + 1],
+                inv_rms[:, b].rearrange("p g c -> p (g c)").unsqueeze(1).to_broadcast([P, PACK, P]),
+                ALU.mult, ALU.mult,
             )
             normed_t = psum.tile([P, PACK, P], F32, name="normed_t%d" % b, tag="block%d" % b)
             for t in range(PACK):
-                nc.tensor.transpose(normed_t[:, t, :], normed[:, t].rearrange("p g c -> p (g c)"), identity[:])
+                nc.tensor.transpose(normed_t[:, t, :], normed[:, t, :], identity[:])
             turned.append(normed_t)
-        wt_codes, wt_plane = quantize(wt_grouped[:], "wt")
+        wt_codes, wt_plane = quantize(wt_grouped, "wt")
 
-        head = psum.tile([P, HIDDEN - P], F32, name="head", tag="head")
-        tail = psum.tile([P, P], F32, name="tail", tag="tail")
+        results = []
+        head = psum.tile([P, half], F32, name="head", tag="head")
         for b in range(BLOCKS):
             activated = held.tile([P, P, PACK], F32, name="activated%d" % b)
             nc.scalar.activation(activated[:], turned[b][:].rearrange("p t r -> p r t"), ACT.Silu)
             ht_grouped = grouped_tile(P, "ht_grouped%d" % b)
             nc.vector.tensor_tensor(ht_grouped[:], activated[:], vs_col[:].unsqueeze(1).to_broadcast([P, P, PACK]), ALU.mult)
-            ht_codes, ht_plane = quantize(ht_grouped[:], "ht%d" % b)
-            target = tail[:] if b == BLOCKS - 1 else head[:, b * P : (b + 1) * P]
+            ht_codes, ht_plane = quantize(ht_grouped, "ht%d" % b)
+            if b < 2:
+                target = head[:, b * P : (b + 1) * P]
+            else:
+                target = psum.tile([P, P], F32, name="result%d" % b, tag=("os_rows", "tail")[b - 2])[:]
+                results.append(target)
             nc.tensor.matmul_mx(out=target, lhsT=wt_codes[:].bitcast(FP8X4), lhsT_scale=wt_plane[:],
                                 rhs=ht_codes[:].bitcast(FP8X4), rhs_scale=ht_plane[:], start=True, stop=True)
 
-        head_out = held.tile([P, HIDDEN - P], F32, name="head_out")
+        head_out = held.tile([P, half], F32, name="head_out")
         nc.scalar.copy(head_out[:], head[:])
-        nc.sync.dma_start(out=out[:, : HIDDEN - P], in_=head_out[:])
-        tail_out = held.tile([P, P], F32, name="tail_out")
-        nc.scalar.copy(tail_out[:], tail[:])
-        nc.scalar.dma_start(out=out[:, HIDDEN - P :], in_=tail_out[:])
+        nc.sync.dma_start(out=out[:, :half], in_=head_out[:])
+        tail_out = held.tile([P, half], F32, name="tail_out")
+        nc.scalar.copy(tail_out[:, :P], results[0])
+        nc.vector.tensor_copy(tail_out[:, P:], results[1])
+        nc.sync.dma_start(out=out[:, half:], in_=tail_out[:])

@@ -143,7 +143,7 @@ def tile_attend_lrscaled_soft_kernel(tc, query, keys_words, keys_scales, tab_wor
             nc.tensor.matmul_mx(out=zh[:], lhsT=w_codes[:].bitcast(FP8X4), lhsT_scale=w_plane[:],
                                 rhs=tab_codes[:].bitcast(FP8X4), rhs_scale=tab_plane[TAB_PLANE:P, :], start=True, stop=True)
             hidden.append(zh)
-            squares = held.tile([P, PAGES, PAGE], F32, name="squares%d" % b)
+            squares = held.tile([P, PAGES, PAGE], F32, name="squares%d" % b, tag="squares%d" % b, align_bytes=64)
             nc.scalar.activation(squares[:].rearrange("p g e -> p (g e)"), zh[:], ACT.Square, scale=0.25)
             nc.vector.tensor_reduce(page_mean[:, b, :], squares[:], AXIS.X, ALU.add)
 
@@ -151,8 +151,6 @@ def tile_attend_lrscaled_soft_kernel(tc, query, keys_words, keys_scales, tab_wor
         pairs_t = psum.tile([P, 2, QUERIES], F32, name="pairs_t", tag="scores")
         for u in range(2):
             nc.tensor.transpose(pairs_t[:, u, :], weight_pairs[:, u : SLOTS // 2 : 2], identity[:])
-        wt_grouped = grouped_tile(QUERIES, "wt_grouped")
-        nc.scalar.copy(wt_grouped[:].bitcast(F32), pairs_t[:].rearrange("p u q -> p q u"))
 
         inv_rms = held.tile([P, BLOCKS, PAGES, PAGE // PACK], F32, name="inv_rms")
         for blocks in (slice(0, BLOCKS - 1), slice(BLOCKS - 1, BLOCKS)):
@@ -176,6 +174,8 @@ def tile_attend_lrscaled_soft_kernel(tc, query, keys_words, keys_scales, tab_wor
             for t in range(PACK):
                 nc.tensor.transpose(normed_t[:, t, :], normed[:, t, :], identity[:])
             turned.append(normed_t)
+        wt_grouped = held.tile([P, QUERIES, PACK], BF16, name="wt_grouped", tag="squares3", align_bytes=64)
+        nc.vector.tensor_copy(wt_grouped[:].bitcast(F32), pairs_t[:].rearrange("p u q -> p q u"))
         wt_codes, wt_plane = quantize(wt_grouped, "wt")
 
         results = []

from contextlib import ExitStack

import concourse.mybir as mybir
from concourse.masks import make_identity

F32 = mybir.dt.float32
BF16 = mybir.dt.bfloat16
I32 = mybir.dt.int32
U32 = mybir.dt.uint32
U16 = mybir.dt.uint16
U8 = mybir.dt.uint8
FP8X4 = mybir.dt.float8_e4m3fn_x4
ACT = mybir.ActivationFunctionType
ALU = mybir.AluOpType
AXIS = mybir.AxisListType

P = 128
PACK = 4
POOL_TOKENS = 2048
SLOTS = 512
HIDDEN = 512
QUERIES = 128
PAGE = 16
PAGES = SLOTS // PAGE
BLOCKS = HIDDEN // P
EPS = 0.1
TAB_PLANE = 4

FLOPS = 2 * 512 * (QUERIES * SLOTS + HIDDEN * SLOTS + QUERIES * HIDDEN)


def tile_attend_lrscaled_soft_kernel(tc, query, keys_words, keys_scales, tab_words, tab_scales, w1, gain, slot_factor, value_scale, offs, out):
    nc = tc.nc
    with ExitStack() as ctx:
        held = ctx.enter_context(tc.tile_pool(name="held", bufs=1))
        psum = ctx.enter_context(tc.psum_pool(name="psum", bufs=1))

        key_bytes = held.tile([P, POOL_TOKENS], U8, name="key_bytes", align_bytes=64)
        tab_bytes = held.tile([P, POOL_TOKENS], U8, name="tab_bytes", tag="tab_bytes", align_bytes=64)
        nc.gpsimd.memset(key_bytes[:, : POOL_TOKENS // 2].bitcast(I32), 0)
        nc.vector.memset(key_bytes[:, POOL_TOKENS // 2 :].bitcast(I32), 0)
        nc.vector.memset(tab_bytes[:].bitcast(I32), 0)

        def load_scale_rows(plane, rows, first, queues):
            for j in range(4):
                queues[j].dma_start(out=plane[first + j : P : 32, :].bitcast(I32), in_=rows[0, j:16:4, :].bitcast(I32))

        def load_words(words, name):
            pool_words = held.tile([P, POOL_TOKENS], U32, name=name, align_bytes=64)
            nc.sync.dma_start(out=pool_words[:].bitcast(I32), in_=words[0].rearrange("p n t -> p (n t)").bitcast(I32))
            return pool_words

        def load_rows(matrix, name):
            raw = held.tile([P, PACK, matrix.shape[1]], F32, name=name, tag=name)
            nc.sync.dma_start(out=raw[:], in_=matrix.rearrange("(p j) c -> p j c", j=PACK))
            return raw

        def load_by_slot(row, name):
            column = held.tile([P, PACK], F32, name=name)
            nc.sync.dma_start(out=column[:], in_=row.rearrange("o (p t) -> (o p) t", t=PACK))
            return column

        half = HIDDEN // 2
        offsets = held.tile([P, SLOTS // 16], U16, name="offsets")
        nc.sync.dma_start(offsets[:], offs)
        q_raw = load_rows(query, "q_raw")
        load_scale_rows(key_bytes, keys_scales, 0, [nc.scalar, nc.scalar, nc.sync, nc.sync])
        key_pool = load_words(keys_words, "key_pool")
        load_scale_rows(tab_bytes, tab_scales, TAB_PLANE, [nc.sync] * 4)
        w_low_raw = load_rows(w1[:, :half], "w_low_raw")
        os_col = load_by_slot(slot_factor, "os_col")
        tab_pool = load_words(tab_words, "tab_pool")
        w_high_raw = load_rows(w1[:, half:], "w_high_raw")
        gain_col = held.tile([P, BLOCKS], F32, name="gain_col")
        with nc.allow_non_contiguous_dma(reason="one gain a partition and block"):
            nc.sync.dma_start(out=gain_col[:], in_=gain.rearrange("(b p) o -> p (b o)", p=P))
        vs_col = load_by_slot(value_scale, "vs_col")

        identity = held.tile([P, P], F32, name="identity")
        make_identity(nc, identity[:])

        def grouped_tile(columns, name):
            return held.tile([P, columns, PACK], BF16, name=name, tag=name, align_bytes=64)

        def interleave(engine_copy, grouped, raw):
            engine_copy(grouped.rearrange("p (c i) j -> p c j i", i=4), raw.rearrange("p j (c i) -> p c j i", i=4))

        def scalar_cast(dst, src):
            nc.scalar.activation(dst, src, ACT.Copy)

        def quantize(grouped, name):
            columns = grouped.shape[1]
            codes = held.tile([P, columns], U32, name=name + "_codes", align_bytes=64)
            plane = held.tile([P, columns], U8, name=name + "_plane", align_bytes=64)
            nc.vector.quantize_mx(out=codes[:].bitcast(FP8X4), scales=plane[:], in_=grouped[:].rearrange("p c j -> p (c j)"))
            return codes, plane

        def gather(pool_tile, dtype, name):
            picked = held.tile([P, SLOTS], dtype, name=name, align_bytes=64)
            nc.vector.tensor_copy(picked[:], pool_tile[:].indirect(offsets[:]))
            return picked

        key_plane = gather(key_bytes, U8, "key_plane")
        q_grouped = grouped_tile(QUERIES, "q_grouped")
        interleave(scalar_cast, q_grouped[:], q_raw[:])
        q_codes, q_plane = quantize(q_grouped, "q")
        key_codes = gather(key_pool, U32, "key_codes")
        scores = psum.tile([P, SLOTS], F32, name="scores", tag="scores")
        nc.tensor.matmul_mx(out=scores[:], lhsT=q_codes[:].bitcast(FP8X4), lhsT_scale=q_plane[:],
                            rhs=key_codes[:].bitcast(FP8X4), rhs_scale=key_plane[:], start=True, stop=True)
        tab_plane = gather(tab_bytes, U8, "tab_plane")

        def quantize_weights(b, engine_copy):
            raw = (w_low_raw, w_high_raw)[b // 2]
            w_grouped = grouped_tile(P, "w_grouped%d" % b)
            interleave(engine_copy, w_grouped[:], raw[:, :, (b % 2) * P : (b % 2 + 1) * P])
            return quantize(w_grouped, "w%d" % b)

        w_mx = [quantize_weights(b, scalar_cast) for b in range(2)]
        neg_max = held.tile([P, 1], F32, name="neg_max", tag="tab_bytes", align_bytes=64)
        nc.vector.tensor_reduce(neg_max[:], scores[:], AXIS.X, ALU.max, negate=True)
        probs = held.tile([P, SLOTS], F32, name="probs", tag="w_low_raw")
        row_sum = held.tile([P, 1], F32, name="row_sum")
        nc.scalar.activation(probs[:], scores[:], ACT.Exp, bias=neg_max[:], accum_out=row_sum[:])
        inv_sum = held.tile([P, 1], F32, name="inv_sum")
        nc.scalar.activation(inv_sum[:], row_sum[:], ACT.Abs_reciprocal_sqrt, scale=row_sum[:])
        os_rows = psum.tile([P, PACK, P], F32, name="os_rows", tag="os_rows")
        for t in range(PACK):
            nc.tensor.transpose(os_rows[:, t, :], os_col[:, t : t + 1].to_broadcast([P, P]), identity[:])

        tab_codes = gather(tab_pool, U32, "tab_codes")
        w_mx.extend(quantize_weights(b, nc.vector.tensor_copy) for b in range(2, BLOCKS))

        weights = held.tile([P, P, PACK], BF16, name="weights", tag="w_grouped2", align_bytes=64)
        nc.vector.scalar_tensor_tensor(weights[:], probs[:].rearrange("q (p t) -> q p t", t=PACK), inv_sum[:],
                                       os_rows[:].rearrange("q t p -> q p t"), ALU.mult, ALU.mult)

        page_mean = held.tile([P, BLOCKS, PAGES], F32, name="page_mean", tag="w_grouped3", align_bytes=64)
        hidden = []
        for b in range(BLOCKS):
            w_codes, w_plane = w_mx[b]
            zh = psum.tile([P, SLOTS], F32, name="zh%d" % b, tag="block%d" % b)
            nc.tensor.matmul_mx(out=zh[:], lhsT=w_codes[:].bitcast(FP8X4), lhsT_scale=w_plane[:],
                                rhs=tab_codes[:].bitcast(FP8X4), rhs_scale=tab_plane[TAB_PLANE:P, :], start=True, stop=True)
            hidden.append(zh)
            squares = held.tile([P, PAGES, PAGE], F32, name="squares%d" % b, tag="squares%d" % b, align_bytes=64)
            nc.scalar.activation(squares[:].rearrange("p g e -> p (g e)"), zh[:], ACT.Square, scale=0.25)
            nc.vector.tensor_reduce(page_mean[:, b, :], squares[:], AXIS.X, ALU.add)

        weight_pairs = weights[:].rearrange("q p t -> q (p t)").bitcast(F32)
        pairs_t = psum.tile([P, 2, QUERIES], F32, name="pairs_t", tag="scores")
        for u in range(2):
            nc.tensor.transpose(pairs_t[:, u, :], weight_pairs[:, u : SLOTS // 2 : 2], identity[:])

        inv_rms = held.tile([P, BLOCKS, PAGES, PAGE // PACK], F32, name="inv_rms")
        for blocks in (slice(0, BLOCKS - 1), slice(BLOCKS - 1, BLOCKS)):
            count = (blocks.stop - blocks.start) * PAGES
            nc.scalar.activation(
                inv_rms[:, blocks].rearrange("p b g c -> p (b g) c"),
                page_mean[:, blocks].rearrange("p b g -> p (b g)").unsqueeze(2).to_broadcast([P, count, PAGE // PACK]),
                ACT.Abs_reciprocal_sqrt, bias=EPS)

        turned = []
        for b in range(BLOCKS):
            normed = held.tile([P, PACK, P], F32, name="normed%d" % b)
            nc.vector.scalar_tensor_tensor(
                normed[:],
                hidden[b][:].rearrange("p (s t) -> p t s", t=PACK),
                gain_col[:, b : b + 1],
                inv_rms[:, b].rearrange("p g c -> p (g c)").unsqueeze(1).to_broadcast([P, PACK, P]),
                ALU.mult, ALU.mult,
            )
            normed_t = psum.tile([P, PACK, P], F32, name="normed_t%d" % b, tag="block%d" % b)
            for t in range(PACK):
                nc.tensor.transpose(normed_t[:, t, :], normed[:, t, :], identity[:])
            turned.append(normed_t)
        wt_grouped = held.tile([P, QUERIES, PACK], BF16, name="wt_grouped", tag="squares3", align_bytes=64)
        nc.vector.tensor_copy(wt_grouped[:].bitcast(F32), pairs_t[:].rearrange("p u q -> p q u"))
        wt_codes, wt_plane = quantize(wt_grouped, "wt")

        results = []
        head = psum.tile([P, half], F32, name="head", tag="head")
        for b in range(BLOCKS):
            activated = held.tile([P, P, PACK], F32, name="activated%d" % b)
            nc.scalar.activation(activated[:], turned[b][:].rearrange("p t r -> p r t"), ACT.Silu)
            ht_grouped = grouped_tile(P, "ht_grouped%d" % b)
            nc.vector.tensor_tensor(ht_grouped[:], activated[:], vs_col[:].unsqueeze(1).to_broadcast([P, P, PACK]), ALU.mult)
            ht_codes, ht_plane = quantize(ht_grouped, "ht%d" % b)
            if b < 2:
                target = head[:, b * P : (b + 1) * P]
            else:
                target = psum.tile([P, P], F32, name="result%d" % b, tag=("os_rows", "tail")[b - 2])[:]
                results.append(target)
            nc.tensor.matmul_mx(out=target, lhsT=wt_codes[:].bitcast(FP8X4), lhsT_scale=wt_plane[:],
                                rhs=ht_codes[:].bitcast(FP8X4), rhs_scale=ht_plane[:], start=True, stop=True)

        head_out = held.tile([P, half], F32, name="head_out")
        nc.scalar.copy(head_out[:], head[:])
        nc.sync.dma_start(out=out[:, :half], in_=head_out[:])
        tail_out = held.tile([P, half], F32, name="tail_out")
        nc.scalar.copy(tail_out[:, :P], results[0])
        nc.vector.tensor_copy(tail_out[:, P:], results[1])
        nc.sync.dma_start(out=out[:, half:], in_=tail_out[:])
